import numpy as np, ml_dtypes
CORES = [35,38,43,46]
N = 4
BF = ml_dtypes.bfloat16
def gentries(a):
    return np.ascontiguousarray(a.reshape(8, 16, -1).transpose(0, 2, 1)).reshape(8, -1)
def gtable(e):
    e = np.asarray(e); return np.ascontiguousarray(e.reshape(8, -1, 16).transpose(0, 2, 1)).reshape(128, -1).astype(np.int32)
L, K, B, RO, CAP = 3584, 896, 4, 12, 128
R = RO // B - 1
def pick(a, v):
    return np.take_along_axis(a, v[:, :, None, :], 3)
def moved(p, c):
    q = p + np.sum(c, axis=2)
    return np.where(q >= 16 * L, q - 16 * L, q)
def sums(C):
    return np.sum(C[..., B - 1::B], axis=2)
def splice(a, cut):
    ids = np.argsort(~cut, axis=2, kind="stable"); n = np.minimum(np.add.reduce(cut.astype(np.int64), axis=2), CAP)
    old = a.reshape(N, 8, 16, K, B); new = old.copy()
    for r in range(N):
        q = (r - 1) % N
        for g in range(8):
            m = min(int(n[r, g]), int(n[q, g]))
            new[r, g][:, ids[r, g, :m]] = old[q, g][:, ids[q, g, :m]]
    return new.reshape(N, 8, 16, L)
def parts(rng):
    x = np.abs(rng.standard_normal((N, 128, L), dtype=np.float32)) * np.exp2(rng.integers(-1, 2, (N, 128, 1)))
    return x, rng.integers(0, 16, (N, 8, 16, L)), rng.integers(0, 16 * L, (N, 8, K)), rng.integers(100, 170, (N, 8, R))
def pack(x, C, p, th):
    return {"tape": np.clip(x, 0, 4).astype(np.float32).astype(BF), "ctl": np.ascontiguousarray(C.reshape(N, 128, L)).astype(np.float32).astype(BF),
            "pos": np.stack([gtable(a) for a in p]), "th": th.astype(np.int32)}
def cols(rng, s):
    c = (s >> 4)[None, :] + (np.argsort(rng.random((16, len(s))), axis=0) < (s & 15)[None, :])
    d = (rng.random((8, len(s))) * (np.minimum(c[0::2], 15 - c[1::2]) + 1)).astype(np.int64)
    c[0::2] -= d; c[1::2] += d
    return c
def tuned(p, C, want):
    C = C.copy(); th = np.zeros((N, 8, R), np.int64)
    for t in range(RO - B):
        j = t % B; c = pick(C, p >> 4)
        C[..., j::B] = (c + C[..., j::B]) & 15
        p = moved(p, c)
        if j == B - 1:
            m = t // B; S = sums(C); D = -np.sort(-S, axis=2); w = want[m]
            a = np.take_along_axis(D, np.maximum(w - 1, 0)[..., None], 2)[..., 0]
            th[:, :, m] = np.where(w == 0, np.minimum(D[..., 0] + 1, 240), a)
            C = splice(C, S >= th[:, :, m, None])
    return th
def setup_inputs(rng):
    x, C, p, th = parts(rng); u = rng.random((N, 8, 1, L))
    C = np.where(u < 0.04, 0, np.where(u > 0.97, 15, C))
    p[..., K - 1] = 16 * L - 1; p[..., 0] = 16 * (L - 1) + rng.integers(0, 16, (N, 8))
    return pack(x, C, p, th)
def setup_inputs_spread(rng):
    x, C, p, th = parts(rng)
    x = x * np.exp2(rng.integers(-3, 4, (N, 1, L))) * (rng.random((N, 1, L)) > 0.0625)
    e = rng.choice(np.array([0.3, 1.0, 3.0]), (N, 8, 1, L), p=np.array([0.25, 0.5, 0.25]))
    C = np.minimum((16 * rng.random((N, 8, 16, L)) ** e).astype(np.int64), 15)
    p = np.where(rng.random((N, 8, K)) < 0.5, p, np.minimum((16 * L * rng.random((N, 8, K)) ** 3).astype(np.int64), 16 * L - 1))
    return pack(x, C, p, rng.integers(40, 200, (N, 8, R)))
def setup_inputs_ends(rng):
    x, C, p, th = parts(rng)
    x = np.where(rng.random(x.shape) < 0.7, np.where(rng.random(x.shape) < 0.5, 0.0, 4.0), x)
    u = rng.random((N, 8, 1, L)); C = np.where(u < 0.3, 0, np.where(u < 0.6, 15, 15 * rng.integers(0, 2, C.shape)))
    p = np.where(rng.random(p.shape) < 0.68, (16 * L - 1) * rng.integers(0, 2, p.shape), p)
    th = np.where(rng.random(th.shape) < 0.85, 240 * rng.integers(0, 2, th.shape), th)
    th[:, :, 0] = 240 * rng.integers(0, 2, (N, 8)); th[:, 0, 0] = 0; th[:, 1, 0] = 240; th[N - 1, 7, 0] = 240; th[0, 7, 0] = 240
    few = np.array([0, 1, 2, 3, K - 2, K - 1]); z = (K // 2) * B + B - 1
    for r in range(N):
        for g in range(8):
            o = (g + r) % 4
            if o == 3: continue
            C[r, g][:, z] = 0; C[r, g][:, few * B + B - 1] = 0 if o == 1 else 15
            p[r, g, few] = 16 * z + rng.integers(0, 16, len(few)); p[r, g, 4] = 0; p[r, g, K - 3] = 16 * L - 1
            if o == 1 and g > 3: th[r, g, 0] = 1
    return pack(x, C, p, th)
def setup_inputs_corners(rng):
    x, C, p, th = parts(rng)
    a = C.copy(); q = p; seen = np.zeros((N, 8, L), bool)
    for t in range(B):
        v = q >> 4; np.put_along_axis(seen, v, True, 2); c = pick(a, v)
        if t < B - 1:
            a[..., t::B] = (c + a[..., t::B]) & 15
            q = moved(q, c)
    free = ~seen[..., B - 1::B]; S = np.sum((c + C[..., B - 1::B]) & 15, axis=2)
    few = [CAP, CAP + 1, 0, CAP - 1, 1, K - 1, 2, K, 3, 256, 255]; o = int(rng.integers(0, 11))
    for r in range(N):
        for g in range(8):
            e = np.flatnonzero(free[r, g]); e = np.concatenate([e[-1:], e[:1], rng.permutation(e[1:-1])]); b = S[r, g][~free[r, g]]
            n = few[((r // 2 if g % 2 == 1 else r) + 3 * g + o) % 11]
            if n >= K - 1: lo = int(np.min(b)); m = len(e) - (K - n)
            else: lo = int(np.max(b)) + 1; m = n
            lo = min(max(lo, 1), 240); coin = rng.random(len(e)) < 0.5
            s = np.where(np.arange(len(e)) < m, np.where(coin, lo, rng.integers(lo, 241, len(e))), np.where(coin, lo - 1, rng.integers(0, lo, len(e))))
            C[r, g][:, e * B + B - 1] = (cols(rng, s) - c[r, g][:, e]) & 15
            th[r, g, 0] = lo
    th[:, 2, 1] = 240; th[:, 6, 1] = 240
    return pack(x, C, p, th)
def setup_inputs_crowd(rng):
    x, C, p, th = parts(rng)
    for r in range(N):
        for g in range(8):
            o = (g + r) % 4; at = int(rng.integers(0, 16 * L))
            if o < 2: p[r, g] = at
            if o == 1: p[r, g, K - 1] = (at + 8 * L) % (16 * L)
            if o == 2:
                own = 16 * B * np.arange(K) + rng.integers(0, 16 * B, K)
                p[r, g] = np.where(rng.random(K) < 0.5, own, rng.choice(np.array([0, 15, 16 * L - 1, 16 * (L - 1), at]), K))
            if o == 3:
                s = int(rng.integers(2, 16)); C[r, g][:, 0] = 0; C[r, g][:, B - 1] = 0; C[r, g][:, L - 1] = cols(rng, np.array([s]))[:, 0]
                p[r, g, 0] = int(rng.integers(0, 16)); p[r, g, np.array([1, K // 2, K - 1])] = 16 * L - s; p[r, g, 2] = 16 * L - s + 1; p[r, g, 3] = 16 * L - s - 1
    return pack(x, C, p, th)
def setup_inputs_calm(rng):
    x, C, p, th = parts(rng)
    for r in range(N):
        C[r, 0] = cols(rng, rng.integers(0, 4, L)); p[r, 0] = (p[r, 0] & -16) + 15 - rng.integers(0, 4, K)
        C[r, 4] = 0; C[r, 4][:, B - 1::B] = cols(rng, rng.integers(0, 4, K))
        p[r, 4] = 16 * (B * rng.integers(0, K, K) + rng.integers(0, B - 1, K)) + rng.integers(0, 16, K)
        for g in (2, 6): C[r, g] = cols(rng, rng.choice(np.array([0, 239, 240]), L))
    few = np.array([1, 0, 2, K - 1, 3, K, CAP, CAP + 1])
    o = np.arange(R)[:, None, None] + np.arange(N)[None, :, None] + 3 * np.arange(8)[None, None, :] + int(rng.integers(0, 8))
    th = tuned(p, C, few[o % 8])
    th[:, 4] = 1 + (np.arange(N)[:, None] + np.arange(R)[None, :] + int(rng.integers(0, 3))) % 3
    return pack(x, C, p, th)
def check_ranges(d):
    bad = []
    for k, lo, hi in (("tape", 0, 4), ("ctl", 0, 15), ("pos", 0, 16 * L - 1), ("th", 0, 240)):
        a = np.asarray(d[k]).astype(np.float64)
        if not (np.min(a) >= lo and np.max(a) <= hi): bad.append("range of " + k)
        elif k == "ctl" and not np.all(a == np.floor(a)): bad.append("whole numbers of ctl")
    return bad
def reference(tape, ctl, pos, th):
    X = tape.astype(np.float64).reshape(N, 8, 16, L); C = ctl.astype(np.float32).astype(np.int64).reshape(N, 8, 16, L)
    p = np.stack([gentries(a) for a in pos]).astype(np.int64); late = np.zeros((N, 8, 16, K))
    for t in range(RO):
        j = t % B; v = p >> 4; w = np.where(v == L - 1, 0, v + 1); part = ((p & 15) * 0.0625)[:, :, None, :]
        a = pick(X, v); s = a + part * (pick(X, w) - a); c = pick(C, v)
        if t > 0: late = np.roll(np.roll(before, 1, axis=0), -t, axis=1)
        X[..., j::B] = np.tanh(0.625 * s + 0.375 * late)
        C[..., j::B] = (c + C[..., j::B]) & 15
        p = moved(p, c); before = s
        if j == B - 1 and t < RO - 1:
            cut = sums(C) >= th[:, :, t // B].astype(np.int64)[:, :, None]
            X = splice(X, cut); C = splice(C, cut)
    return {"yx": X.reshape(N, 128, L).astype(np.float32), "yc": np.sum(C, axis=2).astype(np.float32),
            "yp": np.stack([np.concatenate([gtable(a >> 8), gtable(a & 255)], axis=1) for a in p]).astype(np.float32)}

def check_inputs(d):
    bad = list(check_ranges(d))
    if not bad:
        for name, y in reference(**d).items():
            for q in range(N):
                v = np.abs(np.asarray(y[q], np.float64)); s = np.sqrt(np.mean(v * v))
                if v.max() > 4 * s or s < 2.0 ** -3: bad.append('%s of rank %d is uneven or too small' % (name, q))
    return bad

import math
import numpy as np
from concourse.bass import DstId, RemoteDMATransfer
from concourse.mybir import AluOpType, ActivationFunctionType

OP, AF = AluOpType, ActivationFunctionType

L, K, RO = 3584, 896, 12
PADC = 168
WG = L + PADC
WS = WG + 632
H = 448

CFG = {
    "relay": 1,
    "other_die": True,
    "xch": [[0, 448, 896]] * 11 + [[0, 224, 448, 672, 896]],
    "sch": [[0, 448, 896]] * 12, "zcut": 2, "fold": 1.5, "stage": "g",
    "mode": ["00"] + ["VV"] * 11,
    "conv": [("g", 0, 448), ("g", 448, 896)],
    "nld": 2, "order": "cx", "tld": 4000.0,
    "lz": 5500.0, "lr": 2800.0, "gat": 1.56, "sca": 3.8, "f": 1.25, "pe": 0.417, "dep": 100.0,
    "cpos": [-1, -1, 0.5, 1.5, 3.5, 4.5, 5.5, 6.5, 8.5, 9.5, 10.5, 11.5],
    "cbias": 0.0, "seed": 1, "noise": 0.0, "rounds": 8,
    "anneal": 45000, "heat": 0.002, "aim": 0.8,
    "issue": 300.0, "start": 1500.0, "row": 40.0, "rate": 11.2, "link": 100.0, "rwake": 300.0, "first": 2000.0, "lrate": 14.0,
    "others": [{"gat": 1.1, "sca": 2.0, "f": 1.05, "dep": 60.0, "tld": 3000.0, "start": 1000.0, "rate": 20.0, "link": 200.0}],
}
SPAN = [0.0]
ORDER = []

SCRATCH = {
    "CR": ("sbuf", [128, L], "bfloat16"), "XB": ("sbuf", [128, L + 16], "bfloat16"),
    "C": ("sbuf", [128, WS], "bfloat16"), "X": ("sbuf", [128, WS], "float32"),
    "POS": ("sbuf", [128, 56], "int32"), "P0": ("sbuf", [128, 112], "float32"),
    "TH": ("sbuf", [128, 8], "int32"), "THF": ("sbuf", [128, 8], "float32"),
    "M7": ("sbuf", [128, 56], "bfloat16"), "DG": ("sbuf", [128, 112], "bfloat16"),
    "SEL": ("sbuf", [128, 144], "bfloat16"), "SELT": ("sbuf", [128, 2048], "bfloat16"),
    "RW": ("sbuf", [128, 256], "float32"), "ID32": ("sbuf", [128, 128], "float32"),
    "IDB": ("sbuf", [128, 128], "bfloat16"), "BD8": ("sbuf", [128, 8], "bfloat16"),
    "TRI": ("sbuf", [128, 128], "bfloat16"), "ONES": ("sbuf", [128, 128], "bfloat16"),
    "TWO": ("sbuf", [128, 128], "bfloat16"), "NEG": ("sbuf", [128, 56], "float32"),
    "PIX": ("sbuf", [128, 8], "int32"), "LL": ("sbuf", [128, 8], "uint16"),
    "KT": ("sbuf", [128, 32], "float32"), "DUMP": ("sbuf", [128, 32], "float32"),
    "VI": ("sbuf", [128, 112], "int32"), "OA": ("sbuf", [128, RO * 56], "uint16"),
    "OB": ("sbuf", [128, RO * 56], "uint16"), "PHI": ("sbuf", [128, RO * 56], "bfloat16"),
    "CG": ("sbuf", [128, 2 * K], "bfloat16"), "SG": ("sbuf", [128, K], "bfloat16"),
    "A": ("sbuf", [128, RO * K], "float32"), "D": ("sbuf", [128, K], "float32"),
    "SB": ("sbuf", [128, RO * K], "float32"), "LAND": ("sbuf", [128, (RO - 1) * K], "float32"),
    "Y": ("sbuf", [128, L], "float32"),
    "ARG": ("sbuf", [128, 4 * K], "float32"),
    "CUT": ("sbuf", [128, 56], "bfloat16"), "PI": ("sbuf", [128, 56], "int32"), "LI": ("sbuf", [128, 56], "int32"),
    "BB": ("sbuf", [128, K], "bfloat16"), "GG": ("sbuf", [128, 504], "bfloat16"), "E": ("sbuf", [128, 144], "float32"),
    "Y1": ("sbuf", [128, 32], "float32"), "Y2": ("sbuf", [128, 32], "float32"), "IDS": ("sbuf", [128, 32], "float32"),
    "EV": ("sbuf", [128, 32], "float32"), "O4": ("sbuf", [128, 32], "uint16"),
    "OG": ("sbuf", [128, 16], "uint16"), "OS": ("sbuf", [128, 64], "uint16"),
    "PC": ("sbuf", [128, 2 * 544], "bfloat16"), "LC": ("sbuf", [128, 2 * 544], "bfloat16"),
    "PX": ("sbuf", [128, 2 * 512], "float32"), "LX": ("sbuf", [128, 2 * 512], "float32"),
    "YC": ("sbuf", [128, 224], "float32"), "YP": ("sbuf", [128, 112], "float32"),
    "Q1": ("sbuf", [128, 56], "float32"), "Q2": ("sbuf", [128, 56], "float32"), "QI": ("sbuf", [128, 56], "int32"),
    "PH0": ("psum", [128, 512], "float32"), "PH1": ("psum", [128, 512], "float32"),
    "Z0": ("psum", [128, 512], "float32"), "Z1": ("psum", [128, 512], "float32"),
    "T0": ("psum", [128, 512], "float32"), "T1": ("psum", [128, 512], "float32"),
    "PP": ("psum", [128, 512], "float32"), "RZ": ("psum", [128, 512], "float32"),
}
SEMAPHORES = (["cv", "cs", "cp", "cg", "st", "sent", "lpos", "lth", "lxp"]
              + ["lc%d" % i for i in range(4)] + ["lx%d" % i for i in range(4)]
              + ["z%d_%d%s" % (t, c, x) for t in range(RO - 1) for c in range(4) for x in "ab"]
              + ["rc0", "rc1", "ra0", "ra1", "rb0", "rb1"])
COUNTER = {"v": "cv", "s": "cs", "p": "cp", "g": "cg"}
TWOB = ("bfloat16", "uint16")


def bits(m):
    return bin(m).count("1")


def helper_of(src, dst, T, topo):
    if not CFG["relay"] or topo.chip(src) == topo.chip(dst):
        return None
    can = [h for h in topo.cores_of(src) if T.rank_of(h) is None and topo.may_write(h, dst)]
    far = [h for h in can if (topo.die(h) != topo.die(src)) == CFG["other_die"]]
    return (far or can or [None])[0]


def ways(src, dst, T, topo):
    h = helper_of(src, dst, T, topo)
    direct = topo.mask(src, dst)
    if h is not None:
        return (dst, direct, bits(direct)), (h, topo.mask(src, h) & ~direct, bits(topo.mask(h, dst)))
    es = topo.engines(src, dst)
    low = sum(1 << e for e in es[:len(es) // 2])
    return (dst, low, bits(low)), (dst, direct & ~low, bits(direct & ~low))


def s_pieces(t, kind="sch"):
    b = CFG[kind][t]
    return [(b[i], b[i + 1]) for i in range(len(b) - 1)]


def overlap(a, b):
    if a[2] <= b[1] or b[2] <= a[1]:
        return False
    if a[3] == b[3] and a[3] > 1 and (a[1] - b[1]) % a[3]:
        return False
    return True


def build(g, core, T, topo):
    n = len(T.cores)
    rank = T.rank_of(core)
    nxt, prv = T.cores[(rank + 1) % n], T.cores[(rank - 1) % n]
    ops = []
    stage = [-9.0]
    cyc = 0.83 * CFG["f"]
    V, S, PE = g.vector, g.scalar, g.tensor

    def R(name, a=0, b=None, s=1, p=128):
        if b is None:
            b = SCRATCH[name][1][1]
        return (name, a, b, s, p)

    def ap(r):
        if r[3] == 1:
            return T[r[0]][0:r[4], r[1]:r[2]]
        return T[r[0]][0:r[4], r[1]:r[2]:r[3]]

    def cnt(r):
        return (r[2] - r[1] + r[3] - 1) // r[3]

    def small(*rs):
        return all(SCRATCH[r[0]][2] in TWOB for r in rs)

    def psum(r):
        return SCRATCH[r[0]][0] == "psum"

    def add(eng, cost, fns, rd, wr, sem=None, lat=0.0, tag="x"):
        ops.append({"e": eng, "c": cost, "f": fns, "r": rd, "w": wr, "sem": sem, "lat": lat, "tag": tag,
                    "at": stage[0]})

    def join(k):
        part = ops[-k:]
        del ops[-k + 1:]
        ops[-1].update({"c": sum(o["c"] for o in part), "f": [f for o in part for f in o["f"]],
                        "r": [r for o in part for r in o["r"]], "w": [r for o in part for r in o["w"]]})

    def I(win, off):
        return ("ind", win, off)

    def src(x):
        if x[0] == "ind":
            return ap(x[1]).indirect(ap(x[2])), [x[1], x[2]], True
        return ap(x), [x], False

    def cost(ne, ind_in, ind_out, rate, fix):
        if ind_in:
            return fix + ne * CFG["gat"] * cyc
        if ind_out:
            return fix + ne * CFG["sca"] * cyc
        return max(64, ne * rate) * cyc

    def outp(out):
        if out[0] == "ind":
            return ap(out[1]).indirect(ap(out[2])), [out[1]], [out[2]], True
        return ap(out), [out], [], False

    def ts(out, in0, s1, s2, o0, o1=None, tag="c"):
        a, rd, ind = src(in0)
        rd = list(rd)
        x1 = s1
        if isinstance(s1, tuple):
            rd.append(s1)
            x1 = ap(s1)
        o = ap(out)
        if o1 is None:
            f = lambda: V.tensor_scalar(o, a, x1, None, o0)
        else:
            f = lambda: V.tensor_scalar(o, a, x1, s2, o0, o1)
        add("v", cost(cnt(out), ind, False, 0.5 if small(out, rd[0]) else 1, 50), [f], rd, [out], tag=tag)

    def tt(out, in0, in1, o0, tag="c"):
        a, rd, ind = src(in0)
        o, b = ap(out), ap(in1)
        rate = 1 if psum(in1) or psum(rd[0]) else 2
        add("v", cost(cnt(out), ind, False, rate, 50), [lambda: V.tensor_tensor(o, a, b, o0)], rd + [in1], [out], tag=tag)

    def cp(out, in0, tag="c"):
        o, wr, rd, so = outp(out)
        a = ap(in0)
        add("v", cost(cnt(in0), False, so, 0.5 if small(wr[0], in0) else 1, 50), [lambda: V.tensor_copy(o, a)],
            rd + [in0], wr, tag=tag)

    def ms(out, c):
        o = ap(out)
        add("v", cost(cnt(out), False, False, 0.5 if small(out) else 1, 0), [lambda: V.memset(o, c)], [], [out], tag="k")

    def act(out, in0, fn, bias=None, scale=None, tag="c", extra=0.0):
        a, rd, ind = src(in0)
        o, wr, rd2, so = outp(out)
        kw = {}
        if bias is not None:
            kw["bias"] = bias
        if scale is not None:
            kw["scale"] = scale
        ne = cnt(in0) if so else cnt(out)
        add("s", cost(ne, ind, so, 1, 65) + extra, [lambda: S.activation(o, a, fn, **kw)], rd + rd2, wr, tag=tag)

    def mm(items, tag="c"):
        fns, rd, wr, c = [], [], [], 0.0
        for (out, lt, rh, st, sp) in items:
            fns.append(lambda o=ap(out), a=ap(lt), b=ap(rh), st=st, sp=sp: PE.matmul(o, a, b, st, sp))
            rd += [lt, rh]
            wr.append(out)
            c += max(min(64, cnt(lt)), cnt(rh)) * (1 if small(rh) else 4) * CFG["pe"] * CFG["f"]
        add("p", c, fns, rd, wr, tag=tag)

    def sel(out, in0, pattern, cmp, base, mult, tag="k"):
        o, a = ap(out), ap(in0)
        add("g", 170 + 2 * cnt(out) * cyc, [lambda: g.affine_select(o, a, pattern, cmp, 0.0, base, mult)], [in0], [out], tag=tag)

    def iota(out, pattern, base, mult):
        o = ap(out)
        if SCRATCH[out[0]][2] == "int32":
            f = lambda: g.iota(o, pattern, base, mult)
        else:
            f = lambda: g.iota(o, pattern, base, mult, allow_small_or_imprecise_dtypes=True)
        add("g", 130 + 2 * cnt(out) * cyc, [f], [], [out], tag="k")

    def load(out, in_ap, sem, lat):
        o = ap(out)
        add("y", 60, [lambda: g.sync.dma_start(o, in_ap).then_inc(T.sem[sem], 16)], [], [out], sem=(sem, 16), lat=lat, tag="k")

    stores = [0]

    def store(out_ap, in0):
        a = ap(in0)
        stores[0] += 16
        add("y", 60, [lambda: g.sync.dma_start(out_ap, a).then_inc(T.sem.st, 16)], [in0], [], sem=("st", 0),
            lat=2000 + cnt(in0) * 4 * 128 / 200.0, tag="x")
        d = 8 * (CFG["row"] + cnt(in0) * 4 / CFG["lrate"])
        ops[-1]["dma"] = (1700.0, d, d, 0.0, False)

    sent = [0]
    rid, pid, _se = topo.addr(nxt)
    direct = topo.mask(core, nxt)
    came = bits(topo.mask(prv, core))

    def send(dst, s, sem, split, lat, tag, plus=None):
        row = cnt(s) * (2 if small(s) else 4)
        begin = CFG["start"] - CFG["issue"]
        if not split:
            o, a = ap(dst), ap(s)
            sent[0] += bits(direct)
            f = lambda: g.remote_dma(o, a, T.sem[sem], T.sem.sent, pid, rid, direct)
            add("g", CFG["issue"], [f], [s], [dst], sem=(sem, came), lat=lat, tag=tag)
            ops[-1]["dma"] = (begin, 8 * (CFG["row"] + row / CFG["rate"]),
                              max(16 * (CFG["row"] + row / CFG["rate"]), 128 * row / CFG["link"]), 0.0, True)
            return
        w = cnt(s) // 2
        (to0, m0, _g0), (to1, m1, _g1) = ways(core, nxt, T, topo)
        (_t0, _m0, got0), (_t1, _m1, got1) = ways(prv, core, T, topo)
        both = [s] + ([plus] if plus else [])
        tr = [RemoteDMATransfer(dst_ids=[DstId(rid=topo.addr(to)[0], pnc=topo.addr(to)[1])], dma_engine_mask=m,
                                remote_sem=T.sem[sem + x], srcs=[ap(R(y[0], y[1] + k, y[1] + k + w)) for y in both],
                                dsts=[ap(R(dst[0], dst[1] + k, dst[1] + k + w))], alu_op=1 if plus else 0)
              for (to, m, x, k) in ((to0, m0, "a", 0), (to1, m1, "b", w))]
        sent[0] += bits(m0) + bits(m1)
        chain = R("NEG", 100, 101)
        add("g", CFG["issue"], [lambda: g.remote_dma_fused(tr, local_sem=T.sem.sent)], both,
            [R(dst[0], dst[1], dst[1] + w), chain], sem=(sem + "a", got0), lat=lat - 2500, tag=tag)
        on = 16 * (CFG["row"] + row / 2 / CFG["rate"]) * (CFG["fold"] if plus else 1)
        off = max(on * (1 if CFG["relay"] else 2), 128 * row / (2 if CFG["relay"] else 1) / CFG["link"])
        once = CFG["first"] if sem == "z0_0" else 0.0
        ops[-1]["c"] += once
        ops[-1]["dma"] = (begin, on, off, 0.0, True)
        add("g", 0.0, [], [], [R(dst[0], dst[1] + w, dst[2]), chain], sem=(sem + "b", got1), lat=lat, tag=tag)
        ops[-1]["dma"] = (0.0, 0.0, 0.0, CFG["start"] + off + CFG["rwake"] + once if CFG["relay"] else 0.0, True)

    nld = CFG["nld"]
    w = L // nld
    load(R("POS"), T.pos[:], "lpos", 2000)
    at = 2200
    for which in CFG["order"]:
        if which == "x":
            load(R("XB", L, L + 16), T.tape[:, 0:16], "lxp", at)
        for i in range(nld):
            at += CFG["tld"] / nld
            if which == "c":
                load(R("CR", i * w, (i + 1) * w), T.ctl[:, i * w:(i + 1) * w], "lc%d" % i, at)
            else:
                load(R("XB", i * w, (i + 1) * w), T.tape[:, i * w:(i + 1) * w], "lx%d" % i, at)
    load(R("TH", 0, 2, 1, 8), T.th[:], "lth", at + 100)

    ms(R("ID32"), 1.0)
    sel(R("ID32"), R("ID32"), [[-1, 128]], OP.is_equal, 0, 1)
    ms(R("SEL"), 0.0)
    ms(R("BD8"), 8.0)
    sel(R("BD8"), R("BD8"), [[-16, 8]], OP.is_ge, 0, 1)
    sel(R("BD8"), R("BD8"), [[16, 8]], OP.is_ge, 15, -1)
    ts(R("SEL", 15, 143, 16), R("BD8"), 0.0625, None, OP.mult, tag="k")
    ms(R("IDB"), 1.0)
    sel(R("IDB"), R("IDB"), [[-1, 128]], OP.is_equal, 0, 1)
    ms(R("SELT"), 1.0)
    for hh in range(2):
        sel(R("SELT", hh * 1024, hh * 1024 + 1024), R("SELT", hh * 1024, hh * 1024 + 1024),
            [[-1, 8], [-16, 8], [0, 16]], OP.is_equal, -8 * hh, 1)
    ms(R("RW"), 0.6)
    sel(R("RW"), R("RW"), [[0, 2], [-1, 128]], OP.is_equal, 0, 1)
    ms(R("NEG"), -20.0)
    act(R("GG", 0, 504, 9), R("NEG"), AF.Tanh, tag="k", extra=1300)
    ms(R("ONES"), 1.0)
    ms(R("TWO"), 2.0)
    sel(R("TRI"), R("ONES"), [[1, 128]], OP.is_ge, 0, -1)
    sel(R("M7"), R("ONES", 0, 56), [[0, 7], [-1, 8]], OP.is_equal, 0, 1)
    ms(R("BB", 15, K, 16), 2.0)
    ms(R("C", WG, WS), 0.0)
    ms(R("X", WG, WS), 0.0)
    iota(R("KT"), [[1, 4], [0, 8]], 2 * K, 0)
    iota(R("DUMP"), [[16, 32]], WG, 1)
    iota(R("PIX", 0, 2), [[0, 2]], 0, 1)
    ts(R("PIX", 2, 4), R("PIX", 0, 2), 4, None, OP.arith_shift_right, tag="k")
    ts(R("PIX", 4, 6), R("PIX", 0, 2), 7, None, OP.bitwise_and, tag="k")
    ts(R("PIX", 6, 8), R("PIX", 2, 4), 9.0, None, OP.mult, tag="k")
    tt(R("PIX", 2, 4), R("PIX", 6, 8), R("PIX", 4, 6), OP.add, tag="k")
    for i, k in enumerate((0.0, 1.0, 72.0)):
        ts(R("LL", 2 * i, 2 * i + 2), R("PIX", 2, 4), k, None, OP.add, tag="k")
    ts(R("THF", 0, 2, 1, 8), R("TH", 0, 2, 1, 8), -1.0, 128.0, OP.mult, OP.add, tag="k")
    for m in range(2):
        ts(R("DG", 56 * m, 56 * m + 56, 1, 8), R("M7", 0, 56, 1, 8), R("THF", m, m + 1, 1, 8), None, OP.mult, tag="k")

    ts(R("P0", 0, 56), R("POS"), 0.0625, None, OP.mult)
    for i in range(nld):
        ts(R("C", i * w, (i + 1) * w), R("CR", i * w, (i + 1) * w), 0.125, -1.0, OP.mult, OP.add)
    ts(R("C", L, WG), R("CR", 0, PADC), 0.125, -1.0, OP.mult, OP.add)

    def widen(eng, out, in0):
        if eng == "g":
            sel(out, in0, [[0, cnt(out)]], OP.is_ge, 0, 0, tag="x")
        elif eng == "v":
            cp(out, in0, tag="x")
        else:
            act(out, in0, AF.Copy, tag="x")

    for (eng, a, b) in CFG["conv"]:
        for j in range(1, 4):
            widen(eng, R("X", 4 * a + j, 4 * b, 4), R("XB", 4 * a + j, 4 * b, 4))
    widen("s", R("X", L, WG), R("XB", 0, PADC))

    def moved(t):
        p = R("P0", 56 * (t % 2), 56 * (t % 2) + 56)
        if t > 0:
            tt(p, R("PP", 0, 56), R("P0", 56 - 56 * (t % 2), 112 - 56 * (t % 2)), OP.add)
        return p

    def lists(t):
        p = moved(t)
        vi = R("VI", 56 * (t % 2), 56 * (t % 2) + 56)
        ts(vi, p, -15.0 / 32, None, OP.add)
        ts(R("OA", 56 * t, 56 * t + 56), vi, 8.0 * t, None, OP.add)
        ts(R("OB", 56 * t, 56 * t + 56), vi, 8.0 * t + 1, None, OP.add)
        tt(R("PHI", 56 * t, 56 * t + 56), p, vi, OP.subtract)

    def control(t):
        j = t % 4
        o = K * (t % 2)
        for c in range(2):
            off = R("OA", 56 * t + 28 * c, 56 * t + 28 * c + 28)
            out = R("CG", o + H * c, o + H * c + H)
            if t == 0:
                act(out, I(R("CR"), off), AF.Identity, bias=-1.0, scale=0.125)
            else:
                act(out, I(R("C", 0, WG), off), AF.Copy)
        mm([(R("PP", 0, 56), R("SEL", 15 - q, 143 - q), R("CG", o + q, o + K, 16), q == 0, q == 15) for q in range(16)])
        for c in range(2):
            tb = R("T%d" % c, 0, H)
            mm([(tb, R("IDB"), R("C", 4 * H * c + j, 4 * H * (c + 1), 4), True, False)])
            mm([(tb, R("IDB"), R("CG", o + H * c, o + H * c + H), False, True)])
        for c in range(2):
            tb = R("T%d" % c, 0, H)
            sg = R("SG", H * c, H * c + H)
            act(sg, tb, AF.Sign, bias=0.0625)
            tt(R("C", 4 * H * c + j, 4 * H * (c + 1), 4), tb, sg, OP.subtract)
            if c == 0 and j != 3:
                tt(R("C", L + j, WG, 4), R("T0", 0, PADC // 4), R("SG", 0, PADC // 4), OP.subtract)

    def razor_lists(m):
        mm([(R("RZ", 0, 56), R("ONES", 0, 128, 1, 8), R("DG", 56 * m, 56 * m + 56, 1, 8), True, False)]
           + [(R("RZ", 8 * b, 8 * b + 8), R("C", 512 * b + 3, 512 * b + 512, 4), R("BD8"), False, b == 6) for b in range(7)])
        ts(R("CUT"), R("RZ", 0, 56), 0.0, None, OP.is_ge)
        mm([(R("RZ", 64, 120), R("TRI"), R("CUT"), True, False)]
           + [(R("RZ", 64 + 8 * s, 120), R("ONES"), R("CUT", 0, 56 - 8 * s), False, s == 6) for s in range(1, 7)])
        cp(R("PI"), R("RZ", 64, 120))
        for k in range(1, 9):
            act(R("GG", k, 504, 9), R("RZ", 64, 120), AF.Sign, bias=16.0 * k - 0.5, scale=-1.0)
        join(8)
        ts(R("LI"), R("PI"), 15, None, OP.bitwise_and)
        for q in range(15):
            ts(R("BB", q, K, 16), R("LI"), float(q), 2.0, OP.is_le, OP.mult)
            if q % 5 == 4:
                join(5)
        mm([(R("RZ", 200, 272), R("TWO"), R("GG", 72 * b, 72 * b + 72), b == 0, b == 6) for b in range(7)])
        mm([(R("RZ", 128, 200), R("BB", 128 * b, 128 * b + 128), R("GG", 72 * b, 72 * b + 72), b == 0, b == 6) for b in range(7)])
        act(R("E"), R("RZ", 128, 272), AF.Copy)
        tt(R("Y1"), I(R("E"), R("LL", 0, 2)), R("KT"), OP.subtract)
        tt(R("Y2"), I(R("E"), R("LL", 4, 6)), R("Y1"), OP.subtract)
        tt(R("IDS"), I(R("E"), R("LL", 2, 4)), R("Y2"), OP.add)
        cp(R("O4"), R("IDS"))
        o = 544 * m
        ts(R("PC", o + 512, o + 544), R("IDS"), float(L), None, OP.is_lt)
        act(R("PC", o, o + 512), I(R("C", 0, WG), R("O4")), AF.Copy)
        send(R("LC", o, o + 544), R("PC", o, o + 544), "rc%d" % m, False, CFG["lr"], "c")
        ts(R("OG", 8 * m, 8 * m + 8), R("IDS", 0, 8), 0.25, float(K - 1), OP.mult, OP.min)
        tt(R("Y1"), R("IDS"), R("DUMP"), OP.subtract)
        tt(R("EV"), R("Y1"), R("PC", o + 512, o + 544), OP.mult)
        tt(R("Y2"), R("EV"), R("LC", o + 512, o + 544), OP.mult)
        tt(R("Y1"), R("Y2"), R("DUMP"), OP.add)
        cp(R("OS", 32 * m, 32 * m + 32), R("Y1"))
        cp(I(R("C"), R("OS", 32 * m, 32 * m + 32)), R("LC", o, o + 512))
        cp(R("C", L, WG), R("C", 0, PADC))

    def argbuf(t):
        return ("SB", 0) if t == 0 else ("ARG", K * (t % 4))

    def razor_take(m, planes, sem):
        o = 512 * m
        for j in planes:
            nm, b = argbuf(4 * m + j)
            act(R("PX", o + 128 * j, o + 128 * j + 128), I(R(nm, b, b + K), R("OG", 8 * m, 8 * m + 8)), AF.Identity,
                scale=0.625, tag="x")
        a, b = o + 128 * planes[0], o + 128 * planes[-1] + 128
        send(R("LX", a, b), R("PX", a, b), sem, False, CFG["lr"], "x")

    def razor_put(m, planes):
        o = 512 * m
        act(I(R("X"), R("OS", 32 * m + 8 * planes[0], 32 * m + 8 * planes[-1] + 8)),
            R("LX", o + 128 * planes[0], o + 128 * planes[-1] + 128), AF.Tanh, tag="x")

    def signal(t):
        j = t % 4
        o = K * t
        win = R("XB") if t == 0 else R("X", 0, WG)
        pcs = s_pieces(t, "xch")
        mode = CFG["mode"][t]
        for c in range(2):
            mm([(R("PH%d" % c, q, H, 16), R("SELT", 128 * q, 128 * q + 128),
                 R("PHI", 56 * t + 28 * c, 56 * t + 28 * c + 28), True, True) for q in range(16)], tag="x")
        if t > 0:
            rot = R("RW", 16 * (t % 8), 16 * (t % 8) + 128)
            for c in range(2):
                w = H // CFG["zcut"] if mode[c] == "V" else H
                for a in range(0, H, w):
                    mm([(R("Z%d" % c, a, a + w), rot, R("LAND", K * (t - 1) + H * c + a, K * (t - 1) + H * c + a + w), True,
                         mode[c] == "V")], tag="x")
        for (a, b) in pcs:
            act(R("A", o + a, o + b), I(win, R("OA", 56 * t + a // 16, 56 * t + b // 16)), AF.Copy, tag="x")
        for (a, b) in pcs:
            tt(R("D", a, b), I(win, R("OB", 56 * t + a // 16, 56 * t + b // 16)), R("A", o + a, o + b), OP.subtract, tag="x")
        if j == 3 and t < RO - 1:
            razor_put(t // 4, [0, 1, 2])
        for c in range(2):
            if mode[c] == "A":
                mm([(R("Z%d" % c, 0, H), R("ID32"), R("A", o + H * c, o + H * c + H), False, True)], tag="x")
        for i, (a, b) in enumerate(pcs):
            c = a // H
            ph = R("PH%d" % c, a - H * c, b - H * c)
            sb = R("SB", K * t + a, K * t + b)
            if mode[c] == "A":
                tt(sb, R("D", a, b), ph, OP.mult, tag="x")
            else:
                tt(ph, R("D", a, b), ph, OP.mult, tag="x")
                tt(sb, R("A", o + a, o + b), ph, OP.add, tag="x")
            for k, (a2, b2) in enumerate(s_pieces(t)):
                if t < RO - 1 and b2 == b:
                    send(R("LAND", K * t + a2, K * t + b2), R("SB", K * t + a2, K * t + b2), "z%d_%d" % (t, k), True,
                         CFG["lz"], "x", R("A", o + a2, o + b2) if mode[c] == "A" else None)
        nm, ab = argbuf(t)
        srcs = []
        for (a, b) in pcs:
            c = a // H
            z = R("Z%d" % c, a - H * c, b - H * c)
            sb = R("SB", K * t + a, K * t + b)
            if mode[c] == "P":
                mm([(z, R("ID32"), sb, False, b == H * c + H)], tag="x")
                srcs.append(z)
            else:
                if t > 0:
                    tt(R(nm, ab + a, ab + b), sb, z, OP.add, tag="x")
                srcs.append(R(nm, ab + a, ab + b))
        if j == 2 and t < RO - 2:
            razor_take(t // 4, [0, 1, 2], "ra%d" % (t // 4))
        if j == 3 and t < RO - 1:
            razor_take(t // 4, [3], "rb%d" % (t // 4))
        for (a, b), x in zip(pcs, srcs):
            out = "Y" if CFG["stage"] and t == RO - 1 else "X"
            act(R(out, 4 * a + j, 4 * b, 4), x, AF.Tanh, scale=0.625, tag="x")
            if a == 0 and j != 3:
                act(R("X", L + j, WG, 4), R(x[0], x[1], x[1] + PADC // 4), AF.Tanh, scale=0.625, tag="x")
            if CFG["stage"] and RO - 4 <= t < RO - 1:
                widen(CFG["stage"], R("Y", 4 * a + j, 4 * b, 4), R("X", 4 * a + j, 4 * b, 4))
            if t == RO - 1:
                store(T.yx[:, 4 * a:4 * b], R(out, 4 * a, 4 * b))
        if j == 3 and t < RO - 1:
            razor_put(t // 4, [3])
            act(R("X", L, WG), R("X", 0, PADC), AF.Copy, tag="x")

    lists(0)
    for t in range(RO):
        stage[0] = CFG["cpos"][t]
        control(t)
        if t < RO - 1:
            lists(t + 1)
        if t % 4 == 3 and t < RO - 1:
            razor_lists(t // 4)
    pp = moved(RO)
    ts(R("Q1"), pp, float(L - 8 * RO), -float(L), OP.is_ge, OP.mult)
    tt(R("Q2"), pp, R("Q1"), OP.add)
    ts(R("QI"), R("Q2"), 0.0625, RO / 2 - 255.0 / 512, OP.mult, OP.add)
    cp(R("YP", 0, 56), R("QI"))
    ts(R("Q1"), R("QI"), -16.0, 8.0 * RO, OP.mult, OP.add)
    tt(R("P0", 56, 112), R("Q2"), R("Q1"), OP.add)
    ts(R("YP", 56, 112), R("P0", 56, 112), 16.0, None, OP.mult)
    store(T.yp[:], R("YP"))
    mm([(R("RZ", 0, 224), R("SEL", 15 - b, 143 - b), R("C", 224 * b, 224 * b + 224), b == 0, b == 15) for b in range(16)])
    act(R("YC"), R("RZ", 0, 224), AF.Identity, bias=128.0, scale=16.0)
    store(T.yc[:], R("YC"))
    for t in range(RO):
        stage[0] = float(t)
        signal(t)
    return ops, stores[0], sent[0]


def depend(ops):
    seen = {}
    deps = []
    for i, o in enumerate(ops):
        d = set()
        acc = [(r, False) for r in o["r"]] + [(r, True) for r in o["w"]]
        for (r, w) in acc:
            ps = SCRATCH[r[0]][0] == "psum"
            for (k, r2, w2) in seen.get(r[0], []):
                if k in d:
                    continue
                if ps and ops[k]["e"] != o["e"]:
                    d.add(k)
                elif (w or w2) and overlap(r, r2):
                    d.add(k)
        for (r, w) in set(acc):
            seen.setdefault(r[0], []).append((i, r, w))
        deps.append(d)
    return deps


def replay(order, eng, cost, lat, pred, dma):
    n = len(order)
    da, db = [0.0] * n, [0.0] * n
    fa, fb = [0.0] * 5, [0.0] * 5
    qa = qb = last = 0.0
    for i in order:
        e = eng[i]
        ta, tb = fa[e], fb[e]
        for (k, w) in pred[i]:
            x = da[k] + w
            if x > ta:
                ta = x
            x = db[k] + w
            if x > tb:
                tb = x
        c = cost[i]
        ta += c
        tb += c
        fa[e], fb[e] = ta, tb
        d = dma[i]
        if d is None:
            da[i], db[i] = ta + lat[i], tb + lat[i]
        else:
            qa = max(qa, ta + d[0]) + d[1]
            qb = max(qb, tb + d[0]) + d[2]
            if d[4]:
                da[i], db[i] = qb + d[3], qa
            else:
                da[i], db[i] = qa, qb
                last = max(last, qa, qb)
    return last


def held(order, eng, cost, lat, pred, dma):
    n = len(order)
    done = [[0.0] * n, [0.0] * n]
    back = [[None] * n, [None] * n]
    free = [[(0.0, None)] * 5, [(0.0, None)] * 5]
    q = [0.0, 0.0]
    end = (0.0, 0, 0)
    for i in order:
        for r in range(2):
            t, who = free[r][eng[i]]
            why = (who, True, r)
            for (k, w) in pred[i]:
                x = done[r][k] + w
                if x > t:
                    t, why = x, (k, False, 1 - r if dma[k] and dma[k][4] else r)
            t += cost[i]
            free[r][eng[i]] = (t, i)
            back[r][i] = why
            d = dma[i]
            if d is None:
                done[r][i] = t + lat[i]
            else:
                q[r] = max(q[r], t + d[0]) + d[1 + r]
                if d[4]:
                    done[1 - r][i] = q[r] + d[3] * r
                else:
                    done[r][i] = q[r]
                    end = max(end, (q[r], r, i))
    _t, r, i = end
    arcs = []
    while back[r][i][0] is not None:
        k, wait, r = back[r][i]
        if wait:
            arcs.append((k, i))
        i = k
    return arcs


def anneal(variants, deps, order):
    ops = variants[0][0]
    n = len(ops)
    eng = [o["e"] for o in ops]
    reach = [0] * n
    pred = []
    last = None
    for i in range(n):
        d = set(deps[i])
        if eng[i] == "y" and not ops[i]["r"]:
            if last is not None:
                d.add(last)
            last = i
        keep = []
        for k in sorted(d, reverse=True):
            if not reach[i] >> k & 1:
                keep.append(k)
                reach[i] |= reach[k] | 1 << k
        pred.append([(k, 0.0 if eng[k] == eng[i] == "p" else 1.0) for k in keep])
    for i in range(n):
        pred[i] = [(k, w) for (k, w) in pred[i] if not (eng[k] == eng[i] and ops[k]["sem"] and ops[i]["sem"])]
    num = ["vspgy".index(e) for e in eng]
    sets = [(num, [o["c"] for o in v], [o["lat"] for o in v], [[(k, w * gap) for (k, w) in p] for p in pred],
             [o.get("dma") for o in v]) for (v, gap) in variants]
    base = [replay(order, *x) for x in sets]

    def score(o):
        return sum(replay(o, *x) / b for x, b in zip(sets, base))

    rng = np.random.RandomState(CFG["seed"])
    cur = score(order)
    best = (cur, list(order))
    steps = CFG["anneal"]
    seen = [None, None]
    for it in range(steps):
        if order is not seen[0]:
            seen[:] = [order, held(order, *sets[int(rng.randint(len(sets)))])]
        arcs = seen[1]
        up = rng.rand() < 0.5
        if arcs and rng.rand() < CFG["aim"]:
            i = arcs[int(rng.randint(len(arcs)))][1 if up else 0]
            p = order.index(i)
        else:
            p = int(rng.randint(n))
            i = order[p]
        if eng[i] == "y":
            continue
        hops = 1 + int(rng.randint(3)) * int(rng.randint(3))
        new = list(order)
        if up:
            q = p
            while q > 0 and hops:
                q -= 1
                if eng[order[q]] == eng[i]:
                    hops -= 1
            go = [x for x in order[q:p] if reach[i] >> x & 1]
            stay = [x for x in order[q:p] if not reach[i] >> x & 1]
            new[q:p + 1] = go + [i] + stay
        else:
            q = p
            while q < n - 1 and hops:
                q += 1
                if eng[order[q]] == eng[i]:
                    hops -= 1
            go = [x for x in order[p + 1:q + 1] if reach[x] >> i & 1]
            stay = [x for x in order[p + 1:q + 1] if not reach[x] >> i & 1]
            new[p:q + 1] = stay + [i] + go
        s = score(new)
        heat = CFG["heat"] * (1 - it / steps)
        if s <= cur or rng.rand() < math.exp((cur - s) / heat):
            order, cur = new, s
            if s < best[0]:
                best = (s, list(new))
    SPAN[:] = [round(replay(best[1], *x)) for x in sets]
    return best[1]


def place(ops, order, before, release):
    end = {}
    taken = {}
    for i in order:
        t = max([release[i]] + [end[k] + lag for (k, lag) in before[i]])
        c = ops[i]["c"]
        slots = taken.setdefault(ops[i]["e"], [])
        at = len(slots)
        for x, (a, b) in enumerate(slots):
            if b <= t:
                continue
            if a >= t + c:
                at = x
                break
            t = b
        slots.insert(at, (t, t + c))
        end[i] = t + c
    return end


def schedule(ops, deps):
    n = len(ops)
    before = [[] for _ in range(n)]
    after = [[] for _ in range(n)]
    last = None
    for i in range(n):
        for k in deps[i]:
            lag = ops[k]["lat"] + (0.0 if ops[k]["e"] == ops[i]["e"] == "p" else CFG["dep"])
            if ops[k]["sem"] and ops[i]["sem"] and ops[k]["e"] == ops[i]["e"]:
                lag = 0.0
            before[i].append((k, lag))
            after[k].append((i, lag))
        if ops[i]["e"] == "y" and not ops[i]["r"]:
            if last is not None:
                before[i].append((last, 0.0))
                after[last].append((i, 0.0))
            last = i
    tail = [o["lat"] for o in ops]
    level = [0.0] * n
    seed = CFG["seed"]
    for i in range(n - 1, -1, -1):
        seed = (seed * 1103515245 + 12345) % 2147483648
        level[i] = (ops[i]["c"] * (1 + CFG["noise"] * seed / 2147483648 + (CFG["cbias"] if ops[i]["tag"] == "c" else 0.0))
                    + max([tail[i]] + [level[u] + lag for (u, lag) in after[i]]))
    at = [o["at"] for o in ops]
    for i in range(n - 1, -1, -1):
        at[i] = min([at[i]] + [at[u] for (u, lag) in after[i]])
    order = sorted(range(n), key=lambda i: (at[i], -level[i], i))
    best = None
    for _ in range(CFG["rounds"]):
        end = place(ops, order, before, [0.0] * n)
        span = max(end[i] + tail[i] for i in range(n))
        if best is None or span < best[0]:
            best = (span, sorted(range(n), key=lambda i: (end[i] - ops[i]["c"], i)))
        back = place(ops, sorted(range(n), key=lambda i: (-end[i], -i)), after, tail)
        order = sorted(range(n), key=lambda i: (-back[i], i))
    SPAN[0] = best[0]
    return best[1]


def emit(g, T, ops, deps, order, stores, sent):
    queue = {"v": g.vector, "s": g.scalar, "p": g.tensor, "g": g, "y": g.sync}
    count = {e: 0 for e in COUNTER}
    know = {e: {} for e in queue}
    done = {}
    for i in order:
        o = ops[i]
        e = o["e"]
        need = {}
        for k in deps[i]:
            if (e == "p" and ops[k]["e"] == "p") or (e == "g" and o["sem"] and ops[k]["e"] == "g" and ops[k]["sem"]):
                continue
            sem, val, clock = done[k]
            if sem not in need or need[sem][0] < val:
                need[sem] = (val, clock)
        for sem in sorted(need, key=lambda s: -len(need[s][1])):
            val, clock = need[sem]
            others = [need[s][1].get(sem, 0) for s in need if s != sem]
            if know[e].get(sem, 0) >= val or max(others + [0]) >= val:
                continue
            queue[e].wait_ge(T.sem[sem], val)
        for sem in need:
            val, clock = need[sem]
            know[e][sem] = max(know[e].get(sem, 0), val)
            for s in clock:
                know[e][s] = max(know[e].get(s, 0), clock[s])
        if o["sem"] is None:
            for f in o["f"]:
                f().then_inc(T.sem[COUNTER[e]], 1)
                count[e] += 1
            done[i] = (COUNTER[e], count[e], dict(know[e]))
        else:
            for f in o["f"]:
                f()
            done[i] = (o["sem"][0], o["sem"][1], dict(know[e]) if e == "y" else {})
    for e in COUNTER:
        g.sync.wait_ge(T.sem[COUNTER[e]], count[e])
    g.sync.wait_ge(T.sem.st, stores)
    g.wait_ge(T.sem.sent, sent)


def hand_on(g, core, T, topo, src, dst):
    rid, pid, _se = topo.addr(dst)
    out = topo.mask(core, dst)
    got = bits(topo.mask(src, core) & ~topo.mask(src, dst))
    total = 0
    for t in range(RO - 1):
        for i, (a, b) in enumerate(s_pieces(t)):
            sem = T.sem["z%d_%db" % (t, i)]
            x = T.LAND[:, K * t + (a + b) // 2:K * t + b]
            g.wait_ge(sem, got)
            g.remote_dma(x, x, sem, T.sem.sent, pid, rid, out)
            total += bits(out)
    g.wait_ge(T.sem.sent, total)


def rank_program(g, core, T, topo):
    if T.rank_of(core) is None:
        n = len(T.cores)
        for r in range(n):
            a, b = T.cores[r], T.cores[(r + 1) % n]
            if helper_of(a, b, T, topo) == core:
                hand_on(g, core, T, topo, a, b)
        return
    ops, stores, sent = build(g, core, T, topo)
    deps = depend(ops)
    if not ORDER:
        order = schedule(ops, deps)
        if CFG["anneal"]:
            mid = dict(CFG)
            variants = [(ops, CFG["dep"])]
            for other in CFG["others"]:
                CFG.update(other)
                variants.append((build(g, core, T, topo)[0], CFG["dep"]))
                CFG.update(mid)
            order = anneal(variants, deps, order)
        ORDER.extend(order)
    emit(g, T, ops, deps, ORDER, stores, sent)
